import numpy as np
import ml_dtypes


def mxq(x, axis, fmt="e4m3"):
    dtype, down = {"e4m3": (ml_dtypes.float8_e4m3fn, 7), "e5m2": (ml_dtypes.float8_e5m2, 14)}[fmt]
    v = np.moveaxis(np.asarray(x, np.float32).astype(ml_dtypes.bfloat16).astype(np.float64), axis, -1)
    blocks = v.reshape(v.shape[:-1] + (-1, 32))
    amax = np.abs(blocks).max(-1, keepdims=True)
    byte = np.maximum(np.where(amax > 0, np.frexp(amax)[1] - 1 + 127, 0) - down, 1)
    scale = np.exp2(byte - 127.0)
    codes = (blocks / scale).astype(np.float32).astype(dtype).astype(np.float64)
    return np.moveaxis((codes * scale).reshape(v.shape), -1, axis)


WIDE = False


def mx_kscale(k):
    if not WIDE:
        return np.ones(k)
    levels = np.array([10, -10, 5, -5, 0])
    if k % 512:
        return np.exp2(np.random.permutation(np.resize(levels, k // 32))).repeat(32)
    a = np.empty((k // 512, 16))
    for p in range(k // 512):
        a[p, :8] = np.random.permutation(np.resize(levels, 8))
        for g in range(8):
            far = levels[np.abs(levels - a[p, g]) >= 10]
            a[p, g + 8] = far[np.random.randint(len(far))]
    return np.exp2(a.ravel()).repeat(32)


def f64(x):
    return np.asarray(x).astype(np.float64)


def striped8(idx):
    return np.concatenate([x.reshape(-1, 16).T for x in idx]).astype(np.uint16)


def runs(offs, k):
    lists = np.stack([offs[16 * r : 16 * r + 16].T.reshape(-1) for r in range(8)]).astype(np.int64)
    return lists[np.arange(k) % 512 // 64]


def pack_weight(w):
    k, n = w.shape
    w = f64(np.asarray(w, np.float32).astype(ml_dtypes.bfloat16)).reshape(k // 32, 32, n)
    amax = np.abs(w).max(1)
    byte = np.clip(np.where(amax > 0, np.frexp(amax)[1] - 1 + 127 - 7, 1), 1, 254)
    scaled = (w * np.exp2(127.0 - byte)[:, None, :]).reshape(k, n).astype(np.float32)
    words = np.ascontiguousarray(scaled.reshape(k // 512, 128, 4, n).transpose(0, 1, 3, 2)).astype(ml_dtypes.float8_e4m3fn).view(np.uint8)
    return words, np.ascontiguousarray(byte.astype(np.uint8).reshape(k // 512, 16, n))


def unpack_weight(words, scales):
    g, p, n, _ = words.shape
    vals = np.ascontiguousarray(words).view(ml_dtypes.float8_e4m3fn).astype(np.float64) * np.repeat(np.exp2(scales.astype(np.float64) - 127.0), 8, axis=1)[..., None]
    return vals.transpose(0, 1, 3, 2).reshape(g * 512, n)


E2M1 = np.array([0.0, 0.5, 1.0, 1.5, 2.0, 3.0, 4.0, 6.0, -0.0, -0.5, -1.0, -1.5, -2.0, -3.0, -4.0, -6.0])


def pack_fp4(w):
    k, n = w.shape
    w = f64(np.asarray(w, np.float32).astype(ml_dtypes.bfloat16)).reshape(k // 32, 32, n)
    amax = np.abs(w).max(1)
    mant, ex = np.frexp(amax / 6.0)
    byte = np.clip(np.where(amax > 0, np.where(mant > 0.5, ex, ex - 1) + 127, 1), 1, 254)
    scaled = (w * np.exp2(127.0 - byte)[:, None, :]).reshape(k, n).astype(np.float32)
    c = np.ascontiguousarray(scaled.reshape(k // 512, 128, 4, n).transpose(0, 1, 3, 2)).astype(ml_dtypes.float4_e2m1fn).view(np.uint8) & 0xF
    words = (c[..., 0::2] | (c[..., 1::2] << 4)).reshape(k // 512, 128, 2 * n)
    return np.ascontiguousarray(words), np.ascontiguousarray(byte.astype(np.uint8).reshape(k // 512, 16, n))


def unpack_fp4(words, scales):
    g, _, n = scales.shape
    words = np.ascontiguousarray(words).reshape(g, 128, n, 2)
    nib = np.empty((g, 128, n, 4), np.uint8)
    nib[..., 0::2] = words & 0xF
    nib[..., 1::2] = words >> 4
    vals = E2M1[nib] * np.repeat(np.exp2(scales.astype(np.float64) - 127.0), 8, axis=1)[..., None]
    return vals.transpose(0, 1, 3, 2).reshape(g * 512, n)


def relu(v):
    return np.maximum(v, 0.0)


K, T, S, N, G, H, W, U = 512, 1024, 512, 512, 2048, 512, 256, 1024


def setup_inputs():
    n = np.random.standard_normal
    s = mx_kscale(K)[:, None]
    u = mx_kscale(S)
    packed_xT = pack_weight(n((K, T)) * s)
    packed_dT = pack_weight(n((K, G)) / s)
    packed_w1 = pack_fp4(n((H, N)) / np.sqrt(H) / u[:, None])
    perm = np.stack([np.random.permutation(S) for _ in range(8)])
    return {
        "x_words": packed_xT[0],
        "x_scales": packed_xT[1],
        "d_words": packed_dT[0],
        "d_scales": packed_dT[1],
        "gn": (np.random.uniform(0.5, 1.5, (H, 1)) * u[:, None]).astype(np.float32),
        "w1_words": packed_w1[0],
        "w1_scales": packed_w1[1],
        "offs": striped8(np.random.randint(0, T, (8, S))),
        "ka": striped8(np.random.randint(0, G, (8, H))),
        "kb": striped8(np.random.randint(0, G, (8, H))),
        "n1": striped8(perm[:, :W]),
        "n2": striped8(perm[:, W:]),
        "n3": striped8(np.stack([np.random.permutation(S) for _ in range(8)])),
        "n4": striped8(np.stack([np.random.permutation(U)[:S] for _ in range(8)])),
        "n5": striped8(np.stack([np.random.permutation(S) for _ in range(8)])),
    }


def reference(x_words, x_scales, d_words, d_scales, gn, w1_words, w1_scales, offs, ka, kb, n1, n2, n3, n4, n5):
    d_ka = unpack_weight(d_words, d_scales)[np.arange(K)[:, None], runs(ka, K)]
    xq = unpack_weight(x_words, x_scales)[np.arange(K)[:, None], runs(offs, K)]
    d_kb = unpack_weight(d_words, d_scales)[np.arange(K)[:, None], runs(kb, K)]
    h = 0.0625 * (d_ka.T @ xq + d_kb.T @ xq)
    pa = h[np.arange(H)[:, None], runs(n1, H)]
    pb = h[np.arange(H)[:, None], runs(n2, H)]
    rb = pa - pb
    ra = pa + pb
    ds = np.zeros((H, S))
    ds[np.arange(H)[:, None], runs(n1, H)] = ra
    dt = ds.copy()
    dt[np.arange(H)[:, None], runs(n2, H)] = rb
    z = f64(gn) * (np.maximum(dt, dt[np.arange(H)[:, None], runs(n3, H)]))
    h2 = unpack_fp4(w1_words, w1_scales).T @ mxq(z, 0, "e4m3")
    nw = h2 - (relu(h2[np.arange(N)[:, None], runs(n5, N)]))
    out = np.zeros((N, U))
    out[np.arange(N)[:, None], runs(n4, N)] = nw
    return out

@@ -1,0 +1,237 @@
+from contextlib import ExitStack
+
+import concourse.mybir as mybir
+
+K, T, S, N, G, H, W, U = 512, 1024, 512, 512, 2048, 512, 256, 1024
+FLOPS = 2 * K * H * S * 2 + 2 * H * N * S
+
+F32 = mybir.dt.float32
+BF16 = mybir.dt.bfloat16
+I32 = mybir.dt.int32
+U32 = mybir.dt.uint32
+U16 = mybir.dt.uint16
+U8 = mybir.dt.uint8
+FP8X4 = mybir.dt.float8_e4m3fn_x4
+FP4X4 = mybir.dt.float4_e2m1fn_x4
+ACT = mybir.ActivationFunctionType
+ALU = mybir.AluOpType
+P = 128
+PACK = 4
+HALF = S // 2
+
+
+def tile_picked_haqhaarhpagez_none_p_kernel(
+    tc, x_words, x_scales, d_words, d_scales, gn, w1_words, w1_scales, offs, ka, kb, n1, n2, n3, n4, n5, out
+):
+    nc = tc.nc
+    with ExitStack() as ctx:
+        keep = ctx.enter_context(tc.tile_pool(name="keep", bufs=1))
+        psum = ctx.enter_context(tc.psum_pool(name="psum", bufs=1))
+
+        def tile(shape, dtype, name, tag=None):
+            return keep.tile(shape, dtype, name=name, tag=tag or name, align_bytes=64)
+
+        def load_list(src, name):
+            lst = tile(list(src.shape), U16, name)
+            nc.sync.dma_start(lst[:], src)
+            return lst
+
+        def entries(lst, a, b):
+            return lst[:, a // 16 : b // 16]
+
+        x_bytes = tile([P, T], U8, "x_bytes")
+        d_bytes = tile([P, G], U8, "d_bytes")
+        w_bytes = tile([P, N], U8, "w_bytes")
+        for plane in (x_bytes, d_bytes, w_bytes):
+            nc.vector.memset(plane[:].bitcast(I32), 0)
+        pages = [tile([P, U], F32, "page%d" % t) for t in range(PACK)]
+        nc.vector.memset(pages[0][:].bitcast(I32), 0)
+        for t in range(1, PACK):
+            nc.scalar.activation(pages[t][:], pages[0][:], ACT.Copy)
+
+        offs_l = load_list(offs, "offs_l")
+        ka_l = load_list(ka, "ka_l")
+        kb_l = load_list(kb, "kb_l")
+
+        x_tab = tile([P, T], U32, "x_tab")
+        nc.sync.dma_start(x_tab[:].bitcast(I32), x_words[0].rearrange("p n r -> p (n r)").bitcast(I32))
+        nc.sync.dma_start(x_bytes[0:P:8, :].bitcast(I32), x_scales[0].bitcast(I32))
+        nc.sync.dma_start(d_bytes[0:P:8, :].bitcast(I32), d_scales[0].bitcast(I32))
+        d_tab = tile([P, G], U32, "d_tab")
+        nc.sync.dma_start(d_tab[:].bitcast(I32), d_words[0].rearrange("p n r -> p (n r)").bitcast(I32))
+        n1_l = load_list(n1, "n1_l")
+        n2_l = load_list(n2, "n2_l")
+        w_raw = tile([P, 2 * N], U8, "w_raw")
+        nc.sync.dma_start(w_raw[:].bitcast(I32), w1_words[0].bitcast(I32))
+        n3_l = load_list(n3, "n3_l")
+        gain = tile([P, PACK], F32, "gain")
+        nc.sync.dma_start(gain[:], gn.rearrange("(p t) o -> p (t o)", t=PACK))
+        for q in range(4):
+            nc.sync.dma_start(w_bytes[32 * q : 32 * q + 4, :].bitcast(I32), w1_scales[0][4 * q : 4 * q + 4, :].bitcast(I32))
+        n5_l = load_list(n5, "n5_l")
+        n4_l = load_list(n4, "n4_l")
+
+        got_bytes = tile([P, 3 * S], U8, "got_bytes")
+        nc.vector.tensor_copy(got_bytes[:, 2 * S : 3 * S], x_bytes[:].indirect(offs_l[:]))
+
+        nc.vector.tensor_copy(got_bytes[:, 0:S], d_bytes[:].indirect(ka_l[:]))
+        nc.vector.tensor_copy(got_bytes[:, S : 2 * S], d_bytes[:].indirect(kb_l[:]))
+        planes = tile([P, 3 * S], U8, "planes")
+        nc.vector.tensor_copy(planes[:, 2 * S :].bitcast(I32), got_bytes[:, 2 * S :].bitcast(I32))
+        nc.vector.tensor_copy(
+            planes[:, 0 : 2 * S].rearrange("p (a t m) -> p a t m", a=2, t=PACK),
+            got_bytes[:, 0 : 2 * S].rearrange("p (a m t) -> p a t m", a=2, t=PACK),
+        )
+        for c in range(1, 4):
+            nc.sync.dma_start(planes[c:P:32, :].bitcast(I32), planes[8 * c : P : 32, :].bitcast(I32))
+
+        x_got = tile([P, S], U32, "x_got")
+        nc.vector.tensor_copy(x_got[:], x_tab[:].indirect(offs_l[:]))
+        d_got = [tile([P, H], U32, "d_got%d" % a) for a in range(2)]
+        d_dealt = [tile([P, PACK, P], U32, "d_dealt%d" % a) for a in range(2)]
+
+        def deal(a, t0, t1):
+            nc.vector.tensor_copy(
+                d_dealt[a][:].bitcast(I32)[:, t0:t1, :], d_got[a][:].bitcast(I32).rearrange("p (m t) -> p t m", t=PACK)[:, t0:t1, :]
+            )
+
+        for a, lst in enumerate((ka_l, kb_l)):
+            nc.vector.tensor_copy(d_got[a][:], d_tab[:].indirect(lst[:]))
+            deal(a, 0, 1)
+
+        for a in range(2):
+            deal(a, 1, PACK)
+
+        w_dealt = tile([P, 2 * N], U8, "w_dealt")
+        nc.scalar.copy(
+            w_dealt[:].bitcast(U16).rearrange("p (t m) -> p t m", t=PACK),
+            w_raw[:].bitcast(U16).rearrange("p (m t) -> p t m", t=PACK),
+        )
+        w_plane = tile([P, N], U8, "w_plane", tag="d_got1")
+        nc.vector.tensor_copy(
+            w_plane[:].rearrange("p (t m) -> p t m", t=PACK), w_bytes[:].rearrange("p (m t) -> p t m", t=PACK)
+        )
+
+        h = [tile([P, S], F32, "h%d" % t) for t in range(PACK)]
+        pa = [tile([P, W], F32, "pa%d" % t) for t in range(PACK)]
+        pb = [tile([P, W], F32, "pb%d" % t) for t in range(PACK)]
+        nb = [tile([P, W], F32, "nb%d" % t) for t in range(PACK)]
+        dt = [tile([P, S], F32, "dt%d" % t) for t in range(PACK)]
+        other = [tile([P, S], F32, "other%d" % t) for t in range(PACK)]
+        top = [tile([P, S], F32, "top%d" % t) for t in range(PACK)]
+        pr = [tile([P, 2, HALF, 2], BF16, "pr%d" % hf) for hf in range(2)]
+
+        def first_product(t):
+            acc = psum.tile([P, S], F32, name="acc", tag="bank%d" % t)
+            for a in range(2):
+                nc.tensor.matmul_mx(
+                    out=acc[:],
+                    lhsT=d_dealt[a][:, t, :].bitcast(FP8X4),
+                    lhsT_scale=planes[:, a * S + t * P : a * S + (t + 1) * P],
+                    rhs=x_got[:].bitcast(FP8X4),
+                    rhs_scale=planes[:, 2 * S :],
+                    start=(a == 0),
+                    stop=(a == 1),
+                )
+            nc.scalar.activation(h[t][:], acc[:], ACT.Copy, scale=0.0625)
+            if t == 0:
+                nc.vector.tensor_copy(pa[t][:], h[t][:].indirect(n1_l[:]))
+            else:
+                nc.scalar.activation(pa[t][:], h[t][:].indirect(n1_l[:]), ACT.Copy)
+            nc.scalar.activation(pb[t][:], h[t][:].indirect(n2_l[:]), ACT.Copy)
+
+        def put_sums(t):
+            nc.vector.tensor_tensor(dt[t][:].indirect(n1_l[:]), pa[t][:], pb[t][:], ALU.add)
+
+        def put_differences(t):
+            nc.scalar.activation(nb[t][:], pb[t][:], ACT.Copy, scale=-1.0)
+            nc.vector.tensor_tensor(dt[t][:].indirect(n2_l[:]), pa[t][:], nb[t][:], ALU.add)
+
+        def fetch_other(t):
+            for hf in range(2):
+                look = dt[t][:].indirect(entries(n3_l, hf * HALF, (hf + 1) * HALF))
+                if t == PACK - 1 and hf == 0:
+                    nc.vector.tensor_copy(other[t][:, hf * HALF : (hf + 1) * HALF], look)
+                else:
+                    nc.scalar.activation(other[t][:, hf * HALF : (hf + 1) * HALF], look, ACT.Copy)
+
+        def larger(t):
+            step = HALF if t == PACK - 1 else S
+            for a in range(0, S, step):
+                nc.vector.tensor_tensor(top[t][:, a : a + step], dt[t][:, a : a + step], other[t][:, a : a + step], ALU.max)
+
+        def scale(t):
+            for hf in range(2):
+                nc.scalar.activation(pr[hf][:, t // 2, :, t % 2], top[t][:, hf * HALF : (hf + 1) * HALF], ACT.Copy, scale=gain[:, t : t + 1])
+
+        first_product(0)
+        put_sums(0)
+        put_differences(0)
+        first_product(1)
+        first_product(2)
+        for t in range(1, PACK):
+            put_sums(t)
+            fetch_other(t - 1)
+            larger(t - 1)
+            put_differences(t)
+            if t == 1:
+                first_product(3)
+            else:
+                scale(t - 2)
+
+        scale(PACK - 2)
+        fetch_other(PACK - 1)
+        larger(PACK - 1)
+        scale(PACK - 1)
+
+        woven = []
+        for hf in range(2):
+            woven.append(tile([P, HALF, PACK], BF16, "woven%d" % hf))
+            nc.vector.tensor_copy(
+                woven[hf][:].rearrange("p j t -> p (j t)").bitcast(F32).rearrange("p (j u) -> p j u", u=2),
+                pr[hf][:].rearrange("p u j e -> p u (j e)").bitcast(F32).rearrange("p u j -> p j u"),
+            )
+        z_codes = tile([P, S], U32, "z_codes")
+        z_scales = tile([P, S], U8, "z_scales")
+        for hf in range(2):
+            cols = slice(hf * HALF, (hf + 1) * HALF)
+            nc.vector.quantize_mx(
+                out=z_codes[:, cols].bitcast(FP8X4), scales=z_scales[:, cols], in_=woven[hf][:].rearrange("p j t -> p (j t)")
+            )
+
+        out_rows = out.rearrange("(p t) w -> t p w", t=PACK)
+        for t in range(PACK):
+            h2 = tile([P, S], F32, "h2_%d" % t)
+            pos = tile([P, S], F32, "pos%d" % t)
+            minus = tile([P, S], F32, "minus%d" % t)
+            step = HALF if t == 0 else S
+            accs = []
+            for a in range(0, S, step):
+                cols = slice(a, a + step)
+                acc = psum.tile([P, step], F32, name="acc2", tag="bank%d" % (PACK + t if a == 0 else 0))
+                nc.tensor.matmul_mx(
+                    out=acc[:],
+                    lhsT=w_dealt[:, 2 * P * t : 2 * P * (t + 1)].bitcast(FP4X4),
+                    lhsT_scale=w_plane[:, P * t : P * (t + 1)],
+                    rhs=z_codes[:, cols].bitcast(FP8X4),
+                    rhs_scale=z_scales[:, cols],
+                    start=True,
+                    stop=True,
+                )
+                accs.append(acc)
+                nc.scalar.activation(pos[:, cols], acc[:], ACT.Relu)
+                if a == 0:
+                    nc.scalar.activation(h2[:, cols], acc[:], ACT.Copy)
+            for a in range(0, S, HALF):
+                if a == step:
+                    nc.scalar.activation(h2[:, a:], accs[1][:], ACT.Copy)
+                nc.scalar.activation(
+                    minus[:, a : a + HALF], pos[:].indirect(entries(n5_l, a, a + HALF)), ACT.Copy, scale=-1.0
+                )
+                if (a + HALF) % step == 0:
+                    cols = slice(a + HALF - step, a + HALF)
+                    nc.vector.tensor_tensor(
+                        pages[t][:].indirect(entries(n4_l, cols.start, cols.stop)), h2[:, cols], minus[:, cols], ALU.add
+                    )
+
+            nc.sync.dma_start(out_rows[t], pages[t][:])

@@ -41,73 +41,70 @@ def tile_picked_haqhaarhpagez_none_p_kernel(
 
         x_bytes = tile([P, T], U8, "x_bytes")
         d_bytes = tile([P, G], U8, "d_bytes")
-        w_bytes = tile([P, N], U8, "w_bytes")
-        for plane in (x_bytes, d_bytes, w_bytes):
-            nc.vector.memset(plane[:].bitcast(I32), 0)
+        for plane in (d_bytes, x_bytes):
+            width = plane.shape[1]
+            nc.vector.memset(plane[:, : width // 2].bitcast(I32), 0)
+            nc.gpsimd.memset(plane[:, width // 2 :].bitcast(I32), 0)
+        moved = tile([P, 3 * S], U8, "moved")
+        nc.vector.memset(moved[:].bitcast(I32), 0)
         pages = [tile([P, U], F32, "page%d" % t) for t in range(PACK)]
         nc.vector.memset(pages[0][:].bitcast(I32), 0)
         for t in range(1, PACK):
             nc.scalar.activation(pages[t][:], pages[0][:], ACT.Copy)
 
-        offs_l = load_list(offs, "offs_l")
         ka_l = load_list(ka, "ka_l")
         kb_l = load_list(kb, "kb_l")
+        offs_l = load_list(offs, "offs_l")
+        n1_l = load_list(n1, "n1_l")
 
+        nc.sync.dma_start(d_bytes[0:P:8, :].bitcast(I32), d_scales[0].bitcast(I32))
+        nc.sync.dma_start(x_bytes[0:P:8, :].bitcast(I32), x_scales[0].bitcast(I32))
         x_tab = tile([P, T], U32, "x_tab")
         nc.sync.dma_start(x_tab[:].bitcast(I32), x_words[0].rearrange("p n r -> p (n r)").bitcast(I32))
-        nc.sync.dma_start(x_bytes[0:P:8, :].bitcast(I32), x_scales[0].bitcast(I32))
-        nc.sync.dma_start(d_bytes[0:P:8, :].bitcast(I32), d_scales[0].bitcast(I32))
         d_tab = tile([P, G], U32, "d_tab")
         nc.sync.dma_start(d_tab[:].bitcast(I32), d_words[0].rearrange("p n r -> p (n r)").bitcast(I32))
-        n1_l = load_list(n1, "n1_l")
         n2_l = load_list(n2, "n2_l")
-        w_raw = tile([P, 2 * N], U8, "w_raw")
-        nc.sync.dma_start(w_raw[:].bitcast(I32), w1_words[0].bitcast(I32))
         n3_l = load_list(n3, "n3_l")
         gain = tile([P, PACK], F32, "gain")
         nc.sync.dma_start(gain[:], gn.rearrange("(p t) o -> p (t o)", t=PACK))
-        for q in range(4):
-            nc.sync.dma_start(w_bytes[32 * q : 32 * q + 4, :].bitcast(I32), w1_scales[0][4 * q : 4 * q + 4, :].bitcast(I32))
         n5_l = load_list(n5, "n5_l")
         n4_l = load_list(n4, "n4_l")
 
         got_bytes = tile([P, 3 * S], U8, "got_bytes")
-        nc.vector.tensor_copy(got_bytes[:, 2 * S : 3 * S], x_bytes[:].indirect(offs_l[:]))
 
         nc.vector.tensor_copy(got_bytes[:, 0:S], d_bytes[:].indirect(ka_l[:]))
         nc.vector.tensor_copy(got_bytes[:, S : 2 * S], d_bytes[:].indirect(kb_l[:]))
-        planes = tile([P, 3 * S], U8, "planes")
-        nc.vector.tensor_copy(planes[:, 2 * S :].bitcast(I32), got_bytes[:, 2 * S :].bitcast(I32))
-        nc.vector.tensor_copy(
-            planes[:, 0 : 2 * S].rearrange("p (a t m) -> p a t m", a=2, t=PACK),
-            got_bytes[:, 0 : 2 * S].rearrange("p (a m t) -> p a t m", a=2, t=PACK),
-        )
-        for c in range(1, 4):
-            nc.sync.dma_start(planes[c:P:32, :].bitcast(I32), planes[8 * c : P : 32, :].bitcast(I32))
+        nc.vector.tensor_copy(got_bytes[:, 2 * S : 3 * S], x_bytes[:].indirect(offs_l[:]))
+        for c in range(4):
+            queue = nc.sync if c % 2 == 0 else nc.scalar
+            queue.dma_start(moved[c:P:32, :].bitcast(I32), got_bytes[8 * c : P : 32, :].bitcast(I32))
+        planes = tile([P, 2 * H], U8, "planes")
+        bytes_moved = moved[:, : 2 * H].rearrange("p (a m t) -> p a t m", a=2, t=PACK)
+        bytes_dealt = planes[:].rearrange("p (a t m) -> p a t m", a=2, t=PACK)
 
-        x_got = tile([P, S], U32, "x_got")
+        x_got = tile([P, S], U32, "x_got", tag="x_bytes")
         nc.vector.tensor_copy(x_got[:], x_tab[:].indirect(offs_l[:]))
-        d_got = [tile([P, H], U32, "d_got%d" % a) for a in range(2)]
-        d_dealt = [tile([P, PACK, P], U32, "d_dealt%d" % a) for a in range(2)]
-
-        def deal(a, t0, t1):
-            nc.vector.tensor_copy(
-                d_dealt[a][:].bitcast(I32)[:, t0:t1, :], d_got[a][:].bitcast(I32).rearrange("p (m t) -> p t m", t=PACK)[:, t0:t1, :]
-            )
+        d_got = tile([P, 2 * H], U32, "d_got")
+        d_first = tile([P, 2, P], U32, "d_first")
+        d_rest = tile([P, 2, PACK - 1, P], U32, "d_rest", tag="got_bytes")
+        as_got = d_got[:].bitcast(I32).rearrange("p (a m t) -> p a t m", a=2, t=PACK)
 
         for a, lst in enumerate((ka_l, kb_l)):
-            nc.vector.tensor_copy(d_got[a][:], d_tab[:].indirect(lst[:]))
-            deal(a, 0, 1)
+            nc.vector.tensor_copy(d_got[:, a * H : (a + 1) * H], d_tab[:].indirect(lst[:]))
+            nc.vector.tensor_copy(d_first[:].bitcast(I32)[:, a, :], as_got[:, a, 0, :])
 
-        for a in range(2):
-            deal(a, 1, PACK)
+        nc.vector.tensor_copy(bytes_dealt[:, :, 0, :], bytes_moved[:, :, 0, :])
+        nc.vector.tensor_copy(d_rest[:].bitcast(I32), as_got[:, :, 1:, :])
+        nc.vector.tensor_copy(bytes_dealt[:, :, 1:, :], bytes_moved[:, :, 1:, :])
 
+        w_bytes = tile([P, N], U8, "w_bytes", tag="x_tab")
+        nc.gpsimd.memset(w_bytes[:].bitcast(I32), 0)
+        for q in range(4):
+            nc.sync.dma_start(w_bytes[32 * q : 32 * q + 4, :].bitcast(I32), w1_scales[0][4 * q : 4 * q + 4, :].bitcast(I32))
+        w_raw = tile([P, 2 * N], U8, "w_raw", tag="d_tab")
+        nc.sync.dma_start(w_raw[:].bitcast(I32), w1_words[0].bitcast(I32))
         w_dealt = tile([P, 2 * N], U8, "w_dealt")
-        nc.scalar.copy(
-            w_dealt[:].bitcast(U16).rearrange("p (t m) -> p t m", t=PACK),
-            w_raw[:].bitcast(U16).rearrange("p (m t) -> p t m", t=PACK),
-        )
-        w_plane = tile([P, N], U8, "w_plane", tag="d_got1")
+        w_plane = tile([P, N], U8, "w_plane", tag="d_got")
         nc.vector.tensor_copy(
             w_plane[:].rearrange("p (t m) -> p t m", t=PACK), w_bytes[:].rearrange("p (m t) -> p t m", t=PACK)
         )
@@ -122,22 +119,28 @@ def tile_picked_haqhaarhpagez_none_p_kernel(
         pr = [tile([P, 2, HALF, 2], BF16, "pr%d" % hf) for hf in range(2)]
 
         def first_product(t):
-            acc = psum.tile([P, S], F32, name="acc", tag="bank%d" % t)
-            for a in range(2):
-                nc.tensor.matmul_mx(
-                    out=acc[:],
-                    lhsT=d_dealt[a][:, t, :].bitcast(FP8X4),
-                    lhsT_scale=planes[:, a * S + t * P : a * S + (t + 1) * P],
-                    rhs=x_got[:].bitcast(FP8X4),
-                    rhs_scale=planes[:, 2 * S :],
-                    start=(a == 0),
-                    stop=(a == 1),
-                )
-            nc.scalar.activation(h[t][:], acc[:], ACT.Copy, scale=0.0625)
+            step = HALF if t == 0 else S
+            for c in range(0, S, step):
+                acc = psum.tile([P, step], F32, name="acc", tag="bank%d" % (t if c == 0 else PACK))
+                for a in range(2):
+                    nc.tensor.matmul_mx(
+                        out=acc[:],
+                        lhsT=(d_first[:, a, :] if t == 0 else d_rest[:, a, t - 1, :]).bitcast(FP8X4),
+                        lhsT_scale=planes[:, a * S + t * P : a * S + (t + 1) * P],
+                        rhs=x_got[:, c : c + step].bitcast(FP8X4),
+                        rhs_scale=moved[:, 2 * S + c : 2 * S + c + step],
+                        start=(a == 0),
+                        stop=(a == 1),
+                    )
+                nc.scalar.activation(h[t][:, c : c + step], acc[:], ACT.Copy, scale=0.0625)
+
+        def fetch_a(t):
             if t == 0:
                 nc.vector.tensor_copy(pa[t][:], h[t][:].indirect(n1_l[:]))
             else:
                 nc.scalar.activation(pa[t][:], h[t][:].indirect(n1_l[:]), ACT.Copy)
+
+        def fetch_b(t):
             nc.scalar.activation(pb[t][:], h[t][:].indirect(n2_l[:]), ACT.Copy)
 
         def put_sums(t):
@@ -162,22 +165,40 @@ def tile_picked_haqhaarhpagez_none_p_kernel(
 
         def scale(t):
             for hf in range(2):
-                nc.scalar.activation(pr[hf][:, t // 2, :, t % 2], top[t][:, hf * HALF : (hf + 1) * HALF], ACT.Copy, scale=gain[:, t : t + 1])
+                dst, src = pr[hf][:, t // 2, :, t % 2], top[t][:, hf * HALF : (hf + 1) * HALF]
+                if t == PACK - 1:
+                    nc.vector.tensor_scalar(dst, src, gain[:, t : t + 1], None, ALU.mult)
+                else:
+                    nc.scalar.activation(dst, src, ACT.Copy, scale=gain[:, t : t + 1])
 
         first_product(0)
+        fetch_b(0)
+        fetch_a(0)
+
         put_sums(0)
         put_differences(0)
         first_product(1)
+        fetch_a(1)
+        fetch_b(1)
         first_product(2)
+        fetch_a(2)
         for t in range(1, PACK):
             put_sums(t)
             fetch_other(t - 1)
             larger(t - 1)
             put_differences(t)
             if t == 1:
+                fetch_b(2)
                 first_product(3)
+                fetch_a(3)
+                fetch_b(3)
             else:
                 scale(t - 2)
+            if t == 2:
+                nc.scalar.copy(
+                    w_dealt[:].bitcast(U16).rearrange("p (t m) -> p t m", t=PACK),
+                    w_raw[:].bitcast(U16).rearrange("p (m t) -> p t m", t=PACK),
+                )
 
         scale(PACK - 2)
         fetch_other(PACK - 1)
@@ -225,9 +246,16 @@ def tile_picked_haqhaarhpagez_none_p_kernel(
             for a in range(0, S, HALF):
                 if a == step:
                     nc.scalar.activation(h2[:, a:], accs[1][:], ACT.Copy)
-                nc.scalar.activation(
-                    minus[:, a : a + HALF], pos[:].indirect(entries(n5_l, a, a + HALF)), ACT.Copy, scale=-1.0
-                )
+                if t == 0 and a == 0:
+                    q = HALF // 2
+                    nc.scalar.activation(minus[:, :q], pos[:].indirect(entries(n5_l, 0, q)), ACT.Copy, scale=-1.0)
+                    nc.vector.tensor_scalar(
+                        minus[:, q:HALF], pos[:].indirect(entries(n5_l, q, HALF)), -1.0, 0.0, ALU.mult, ALU.add
+                    )
+                else:
+                    nc.scalar.activation(
+                        minus[:, a : a + HALF], pos[:].indirect(entries(n5_l, a, a + HALF)), ACT.Copy, scale=-1.0
+                    )
                 if (a + HALF) % step == 0:
                     cols = slice(a + HALF - step, a + HALF)
                     nc.vector.tensor_tensor(

@@ -151,12 +151,13 @@ def tile_picked_haqhaarhpagez_none_p_kernel(
             nc.vector.tensor_tensor(dt[t][:].indirect(n2_l[:]), pa[t][:], nb[t][:], ALU.add)
 
         def fetch_other(t):
-            for hf in range(2):
-                look = dt[t][:].indirect(entries(n3_l, hf * HALF, (hf + 1) * HALF))
-                if t == PACK - 1 and hf == 0:
-                    nc.vector.tensor_copy(other[t][:, hf * HALF : (hf + 1) * HALF], look)
+            step = HALF // 2 if t == PACK - 1 else HALF
+            for i, c in enumerate(range(0, S, step)):
+                look = dt[t][:].indirect(entries(n3_l, c, c + step))
+                if t == PACK - 1 and i % 2 == 0:
+                    nc.vector.tensor_copy(other[t][:, c : c + step], look)
                 else:
-                    nc.scalar.activation(other[t][:, hf * HALF : (hf + 1) * HALF], look, ACT.Copy)
+                    nc.scalar.activation(other[t][:, c : c + step], look, ACT.Copy)
 
         def larger(t):
             step = HALF if t == PACK - 1 else S
@@ -240,9 +241,11 @@ def tile_picked_haqhaarhpagez_none_p_kernel(
                     stop=True,
                 )
                 accs.append(acc)
-                nc.scalar.activation(pos[:, cols], acc[:], ACT.Relu)
                 if a == 0:
+                    nc.scalar.activation(pos[:, cols], acc[:], ACT.Relu)
                     nc.scalar.activation(h2[:, cols], acc[:], ACT.Copy)
+                else:
+                    nc.vector.tensor_scalar(pos[:, cols], acc[:], 0.0, None, ALU.max)
             for a in range(0, S, HALF):
                 if a == step:
                     nc.scalar.activation(h2[:, a:], accs[1][:], ACT.Copy)
@@ -262,4 +265,8 @@ def tile_picked_haqhaarhpagez_none_p_kernel(
                         pages[t][:].indirect(entries(n4_l, cols.start, cols.stop)), h2[:, cols], minus[:, cols], ALU.add
                     )
 
-            nc.sync.dma_start(out_rows[t], pages[t][:])
+            if t < PACK - 1:
+                nc.sync.dma_start(out_rows[t], pages[t][:])
+            else:
+                nc.sync.dma_start(out_rows[t][:, : U // 2], pages[t][:, : U // 2])
+                nc.scalar.dma_start(out_rows[t][:, U // 2 :], pages[t][:, U // 2 :])

from contextlib import ExitStack

import concourse.mybir as mybir

K, T, S, N, G, H, W, U = 512, 1024, 512, 512, 2048, 512, 256, 1024
FLOPS = 2 * K * H * S * 2 + 2 * H * N * S

F32 = mybir.dt.float32
BF16 = mybir.dt.bfloat16
I32 = mybir.dt.int32
U32 = mybir.dt.uint32
U16 = mybir.dt.uint16
U8 = mybir.dt.uint8
FP8X4 = mybir.dt.float8_e4m3fn_x4
FP4X4 = mybir.dt.float4_e2m1fn_x4
ACT = mybir.ActivationFunctionType
ALU = mybir.AluOpType
P = 128
PACK = 4
HALF = S // 2


def tile_picked_haqhaarhpagez_none_p_kernel(
    tc, x_words, x_scales, d_words, d_scales, gn, w1_words, w1_scales, offs, ka, kb, n1, n2, n3, n4, n5, out
):
    nc = tc.nc
    with ExitStack() as ctx:
        keep = ctx.enter_context(tc.tile_pool(name="keep", bufs=1))
        psum = ctx.enter_context(tc.psum_pool(name="psum", bufs=1))

        def tile(shape, dtype, name, tag=None):
            return keep.tile(shape, dtype, name=name, tag=tag or name, align_bytes=64)

        def load_list(src, name):
            lst = tile(list(src.shape), U16, name)
            nc.sync.dma_start(lst[:], src)
            return lst

        def entries(lst, a, b):
            return lst[:, a // 16 : b // 16]

        x_bytes = tile([P, T], U8, "x_bytes")
        d_bytes = tile([P, G], U8, "d_bytes")
        for plane in (d_bytes, x_bytes):
            width = plane.shape[1]
            nc.vector.memset(plane[:, : width // 2].bitcast(I32), 0)
            nc.gpsimd.memset(plane[:, width // 2 :].bitcast(I32), 0)
        moved = tile([P, 3 * S], U8, "moved")
        nc.vector.memset(moved[:].bitcast(I32), 0)
        pages = [tile([P, U], F32, "page%d" % t) for t in range(PACK)]
        nc.vector.memset(pages[0][:].bitcast(I32), 0)
        for t in range(1, PACK):
            nc.scalar.activation(pages[t][:], pages[0][:], ACT.Copy)

        ka_l = load_list(ka, "ka_l")
        kb_l = load_list(kb, "kb_l")
        offs_l = load_list(offs, "offs_l")
        n1_l = load_list(n1, "n1_l")

        nc.sync.dma_start(d_bytes[0:P:8, :].bitcast(I32), d_scales[0].bitcast(I32))
        nc.sync.dma_start(x_bytes[0:P:8, :].bitcast(I32), x_scales[0].bitcast(I32))
        x_tab = tile([P, T], U32, "x_tab")
        nc.sync.dma_start(x_tab[:].bitcast(I32), x_words[0].rearrange("p n r -> p (n r)").bitcast(I32))
        d_tab = tile([P, G], U32, "d_tab")
        nc.sync.dma_start(d_tab[:].bitcast(I32), d_words[0].rearrange("p n r -> p (n r)").bitcast(I32))
        n2_l = load_list(n2, "n2_l")
        n3_l = load_list(n3, "n3_l")
        gain = tile([P, PACK], F32, "gain")
        nc.sync.dma_start(gain[:], gn.rearrange("(p t) o -> p (t o)", t=PACK))
        n5_l = load_list(n5, "n5_l")
        n4_l = load_list(n4, "n4_l")

        got_bytes = tile([P, 3 * S], U8, "got_bytes")

        nc.vector.tensor_copy(got_bytes[:, 0:S], d_bytes[:].indirect(ka_l[:]))
        nc.vector.tensor_copy(got_bytes[:, S : 2 * S], d_bytes[:].indirect(kb_l[:]))
        nc.vector.tensor_copy(got_bytes[:, 2 * S : 3 * S], x_bytes[:].indirect(offs_l[:]))
        for c in range(4):
            queue = nc.sync if c % 2 == 0 else nc.scalar
            queue.dma_start(moved[c:P:32, :].bitcast(I32), got_bytes[8 * c : P : 32, :].bitcast(I32))
        planes = tile([P, 2 * H], U8, "planes")
        bytes_moved = moved[:, : 2 * H].rearrange("p (a m t) -> p a t m", a=2, t=PACK)
        bytes_dealt = planes[:].rearrange("p (a t m) -> p a t m", a=2, t=PACK)

        x_got = tile([P, S], U32, "x_got", tag="x_bytes")
        nc.vector.tensor_copy(x_got[:], x_tab[:].indirect(offs_l[:]))
        d_got = tile([P, 2 * H], U32, "d_got")
        d_first = tile([P, 2, P], U32, "d_first")
        d_rest = tile([P, 2, PACK - 1, P], U32, "d_rest", tag="got_bytes")
        as_got = d_got[:].bitcast(I32).rearrange("p (a m t) -> p a t m", a=2, t=PACK)

        for a, lst in enumerate((ka_l, kb_l)):
            nc.vector.tensor_copy(d_got[:, a * H : (a + 1) * H], d_tab[:].indirect(lst[:]))
            nc.vector.tensor_copy(d_first[:].bitcast(I32)[:, a, :], as_got[:, a, 0, :])

        nc.vector.tensor_copy(bytes_dealt[:, :, 0, :], bytes_moved[:, :, 0, :])
        nc.vector.tensor_copy(d_rest[:].bitcast(I32), as_got[:, :, 1:, :])
        nc.vector.tensor_copy(bytes_dealt[:, :, 1:, :], bytes_moved[:, :, 1:, :])

        w_bytes = tile([P, N], U8, "w_bytes", tag="x_tab")
        nc.gpsimd.memset(w_bytes[:].bitcast(I32), 0)
        for q in range(4):
            nc.sync.dma_start(w_bytes[32 * q : 32 * q + 4, :].bitcast(I32), w1_scales[0][4 * q : 4 * q + 4, :].bitcast(I32))
        w_raw = tile([P, 2 * N], U8, "w_raw", tag="d_tab")
        nc.sync.dma_start(w_raw[:].bitcast(I32), w1_words[0].bitcast(I32))
        w_dealt = tile([P, 2 * N], U8, "w_dealt")
        w_plane = tile([P, N], U8, "w_plane", tag="d_got")
        nc.vector.tensor_copy(
            w_plane[:].rearrange("p (t m) -> p t m", t=PACK), w_bytes[:].rearrange("p (m t) -> p t m", t=PACK)
        )

        h = [tile([P, S], F32, "h%d" % t) for t in range(PACK)]
        pa = [tile([P, W], F32, "pa%d" % t) for t in range(PACK)]
        pb = [tile([P, W], F32, "pb%d" % t) for t in range(PACK)]
        nb = [tile([P, W], F32, "nb%d" % t) for t in range(PACK)]
        dt = [tile([P, S], F32, "dt%d" % t) for t in range(PACK)]
        other = [tile([P, S], F32, "other%d" % t) for t in range(PACK)]
        top = [tile([P, S], F32, "top%d" % t) for t in range(PACK)]
        pr = [tile([P, 2, HALF, 2], BF16, "pr%d" % hf) for hf in range(2)]

        def first_product(t):
            step = HALF if t == 0 else S
            for c in range(0, S, step):
                acc = psum.tile([P, step], F32, name="acc", tag="bank%d" % (t if c == 0 else PACK))
                for a in range(2):
                    nc.tensor.matmul_mx(
                        out=acc[:],
                        lhsT=(d_first[:, a, :] if t == 0 else d_rest[:, a, t - 1, :]).bitcast(FP8X4),
                        lhsT_scale=planes[:, a * S + t * P : a * S + (t + 1) * P],
                        rhs=x_got[:, c : c + step].bitcast(FP8X4),
                        rhs_scale=moved[:, 2 * S + c : 2 * S + c + step],
                        start=(a == 0),
                        stop=(a == 1),
                    )
                nc.scalar.activation(h[t][:, c : c + step], acc[:], ACT.Copy, scale=0.0625)

        def fetch_a(t):
            if t == 0:
                nc.vector.tensor_copy(pa[t][:], h[t][:].indirect(n1_l[:]))
            else:
                nc.scalar.activation(pa[t][:], h[t][:].indirect(n1_l[:]), ACT.Copy)

        def fetch_b(t):
            nc.scalar.activation(pb[t][:], h[t][:].indirect(n2_l[:]), ACT.Copy)

        def put_sums(t):
            nc.vector.tensor_tensor(dt[t][:].indirect(n1_l[:]), pa[t][:], pb[t][:], ALU.add)

        def put_differences(t):
            nc.scalar.activation(nb[t][:], pb[t][:], ACT.Copy, scale=-1.0)
            nc.vector.tensor_tensor(dt[t][:].indirect(n2_l[:]), pa[t][:], nb[t][:], ALU.add)

        def fetch_other(t):
            step = HALF // 2 if t == PACK - 1 else HALF
            for i, c in enumerate(range(0, S, step)):
                look = dt[t][:].indirect(entries(n3_l, c, c + step))
                if t == PACK - 1 and i % 2 == 0:
                    nc.vector.tensor_copy(other[t][:, c : c + step], look)
                else:
                    nc.scalar.activation(other[t][:, c : c + step], look, ACT.Copy)

        def larger(t):
            step = HALF if t == PACK - 1 else S
            for a in range(0, S, step):
                nc.vector.tensor_tensor(top[t][:, a : a + step], dt[t][:, a : a + step], other[t][:, a : a + step], ALU.max)

        def scale(t):
            for hf in range(2):
                dst, src = pr[hf][:, t // 2, :, t % 2], top[t][:, hf * HALF : (hf + 1) * HALF]
                if t == PACK - 1:
                    nc.vector.tensor_scalar(dst, src, gain[:, t : t + 1], None, ALU.mult)
                else:
                    nc.scalar.activation(dst, src, ACT.Copy, scale=gain[:, t : t + 1])

        first_product(0)
        fetch_b(0)
        fetch_a(0)

        put_sums(0)
        put_differences(0)
        first_product(1)
        fetch_a(1)
        fetch_b(1)
        first_product(2)
        fetch_a(2)
        for t in range(1, PACK):
            put_sums(t)
            fetch_other(t - 1)
            larger(t - 1)
            put_differences(t)
            if t == 1:
                fetch_b(2)
                first_product(3)
                fetch_a(3)
                fetch_b(3)
            else:
                scale(t - 2)
            if t == 2:
                nc.scalar.copy(
                    w_dealt[:].bitcast(U16).rearrange("p (t m) -> p t m", t=PACK),
                    w_raw[:].bitcast(U16).rearrange("p (m t) -> p t m", t=PACK),
                )

        scale(PACK - 2)
        fetch_other(PACK - 1)
        larger(PACK - 1)
        scale(PACK - 1)

        woven = []
        for hf in range(2):
            woven.append(tile([P, HALF, PACK], BF16, "woven%d" % hf))
            nc.vector.tensor_copy(
                woven[hf][:].rearrange("p j t -> p (j t)").bitcast(F32).rearrange("p (j u) -> p j u", u=2),
                pr[hf][:].rearrange("p u j e -> p u (j e)").bitcast(F32).rearrange("p u j -> p j u"),
            )
        z_codes = tile([P, S], U32, "z_codes")
        z_scales = tile([P, S], U8, "z_scales")
        for hf in range(2):
            cols = slice(hf * HALF, (hf + 1) * HALF)
            nc.vector.quantize_mx(
                out=z_codes[:, cols].bitcast(FP8X4), scales=z_scales[:, cols], in_=woven[hf][:].rearrange("p j t -> p (j t)")
            )

        out_rows = out.rearrange("(p t) w -> t p w", t=PACK)
        for t in range(PACK):
            h2 = tile([P, S], F32, "h2_%d" % t)
            pos = tile([P, S], F32, "pos%d" % t)
            minus = tile([P, S], F32, "minus%d" % t)
            step = HALF if t == 0 else S
            accs = []
            for a in range(0, S, step):
                cols = slice(a, a + step)
                acc = psum.tile([P, step], F32, name="acc2", tag="bank%d" % (PACK + t if a == 0 else 0))
                nc.tensor.matmul_mx(
                    out=acc[:],
                    lhsT=w_dealt[:, 2 * P * t : 2 * P * (t + 1)].bitcast(FP4X4),
                    lhsT_scale=w_plane[:, P * t : P * (t + 1)],
                    rhs=z_codes[:, cols].bitcast(FP8X4),
                    rhs_scale=z_scales[:, cols],
                    start=True,
                    stop=True,
                )
                accs.append(acc)
                if a == 0:
                    nc.scalar.activation(pos[:, cols], acc[:], ACT.Relu)
                    nc.scalar.activation(h2[:, cols], acc[:], ACT.Copy)
                else:
                    nc.vector.tensor_scalar(pos[:, cols], acc[:], 0.0, None, ALU.max)
            for a in range(0, S, HALF):
                if a == step:
                    nc.scalar.activation(h2[:, a:], accs[1][:], ACT.Copy)
                if t == 0 and a == 0:
                    q = HALF // 2
                    nc.scalar.activation(minus[:, :q], pos[:].indirect(entries(n5_l, 0, q)), ACT.Copy, scale=-1.0)
                    nc.vector.tensor_scalar(
                        minus[:, q:HALF], pos[:].indirect(entries(n5_l, q, HALF)), -1.0, 0.0, ALU.mult, ALU.add
                    )
                else:
                    nc.scalar.activation(
                        minus[:, a : a + HALF], pos[:].indirect(entries(n5_l, a, a + HALF)), ACT.Copy, scale=-1.0
                    )
                if (a + HALF) % step == 0:
                    cols = slice(a + HALF - step, a + HALF)
                    nc.vector.tensor_tensor(
                        pages[t][:].indirect(entries(n4_l, cols.start, cols.stop)), h2[:, cols], minus[:, cols], ALU.add
                    )

            if t < PACK - 1:
                nc.sync.dma_start(out_rows[t], pages[t][:])
            else:
                nc.sync.dma_start(out_rows[t][:, : U // 2], pages[t][:, : U // 2])
                nc.scalar.dma_start(out_rows[t][:, U // 2 :], pages[t][:, U // 2 :])
